import numpy as np
import ml_dtypes


def mxq(x, axis, fmt="e4m3"):
    dtype, down = {"e4m3": (ml_dtypes.float8_e4m3fn, 7), "e5m2": (ml_dtypes.float8_e5m2, 14)}[fmt]
    v = np.moveaxis(np.asarray(x, np.float32).astype(ml_dtypes.bfloat16).astype(np.float64), axis, -1)
    blocks = v.reshape(v.shape[:-1] + (-1, 32))
    amax = np.abs(blocks).max(-1, keepdims=True)
    byte = np.maximum(np.where(amax > 0, np.frexp(amax)[1] - 1 + 127, 0) - down, 1)
    scale = np.exp2(byte - 127.0)
    codes = (blocks / scale).astype(np.float32).astype(dtype).astype(np.float64)
    return np.moveaxis((codes * scale).reshape(v.shape), -1, axis)


WIDE = False


def mx_kscale(k):
    if not WIDE:
        return np.ones(k)
    levels = np.array([10, -10, 5, -5, 0])
    if k % 512:
        return np.exp2(np.random.permutation(np.resize(levels, k // 32))).repeat(32)
    a = np.empty((k // 512, 16))
    for p in range(k // 512):
        a[p, :8] = np.random.permutation(np.resize(levels, 8))
        for g in range(8):
            far = levels[np.abs(levels - a[p, g]) >= 10]
            a[p, g + 8] = far[np.random.randint(len(far))]
    return np.exp2(a.ravel()).repeat(32)


def f64(x):
    return np.asarray(x).astype(np.float64)


def striped(idx):
    return np.tile(np.asarray(idx).reshape(-1, 16).T, (8, 1)).astype(np.uint16)


def unstriped(offs):
    return offs[:16].T.reshape(-1).astype(np.int64)


B, N, T, D, DV, NQ = 2, 512, 2048, 512, 256, 512


def setup_inputs():
    n = np.random.standard_normal
    idx = np.random.permutation(T)[:B * N]
    s = mx_kscale(D)[:, None]
    u = np.ones(T)
    u[idx] = mx_kscale(B * N)
    r = np.random.uniform(0.5, 2.0, T)
    qidx = idx
    k = n((D, T)) / s
    v = n((DV, T)) / (u * r)
    return {
        "xq": (n((D, T)) * s * (0.60 / np.sqrt(D))).astype(np.float32),
        "kT": k.astype(np.float32),
        "vT": v.astype(np.float32),
        "vs": np.tile(u * r, (128, 1)).astype(np.float32),
        "offs": striped(idx),
        "qoffs": striped(qidx),
    }


def reference(xq, kT, vT, vs, offs, qoffs):
    idx = unstriped(offs)
    k = f64(kT)
    v = f64(vT)
    pick = lambda x: x[:, idx].reshape(x.shape[0], B, N).transpose(1, 0, 2)
    q = f64(xq)[:, unstriped(qoffs)].reshape(D, B, NQ).transpose(1, 0, 2)
    score = mxq(q, 1, "e4m3").transpose(0, 2, 1) @ mxq(pick(k), 1, "e4m3")
    m = score.max(-1, keepdims=True)
    p = np.exp(score - m)
    total = p.sum(-1, keepdims=True)
    w = p * pick(f64(vs))[:, :1, :]
    y = mxq(w, 2, "e4m3") @ mxq(pick(v).transpose(0, 2, 1), 1, "e4m3")
    y = y / total
    out = np.zeros((DV, T))
    out[:, unstriped(qoffs)] = y.transpose(2, 0, 1).reshape(-1, B * NQ)
    return out

@@ -1,0 +1,255 @@
+from contextlib import ExitStack
+
+import concourse.mybir as mybir
+from concourse.masks import make_identity
+
+F32 = mybir.dt.float32
+BF16 = mybir.dt.bfloat16
+U32 = mybir.dt.uint32
+U16 = mybir.dt.uint16
+U8 = mybir.dt.uint8
+FP8X4 = mybir.dt.float8_e4m3fn_x4
+MULT = mybir.AluOpType.mult
+MAX = mybir.AluOpType.max
+AX = mybir.AxisListType.X
+EXP = mybir.ActivationFunctionType.Exp
+COPY = mybir.ActivationFunctionType.Copy
+
+P = 128
+B, N, T, D, DV = 2, 512, 2048, 512, 256
+FLOPS = 2 * B * N * N * (D + DV)
+LIST = N // 16
+
+EVEN = ((0, 1024, 832), (1024, 1024, 832))
+FIRST = ((0, 512, 352), (512, 512, 416), (1024, 1024, 832))
+LAST = ((0, 1024, 832), (1024, 512, 416), (1536, 256, 160), (1792, 256, 96))
+
+
+def tile_attend_cluster_self_kernel(tc, xq, kT, vT, vs, offs, qoffs, out):
+    nc = tc.nc
+    with ExitStack() as ctx:
+        keep = ctx.enter_context(tc.tile_pool(name="keep", bufs=1))
+        work = ctx.enter_context(tc.tile_pool(name="work", bufs=3))
+        psum_s = ctx.enter_context(tc.psum_pool(name="psum_s", bufs=4))
+        psum_p = ctx.enter_context(tc.psum_pool(name="psum_p", bufs=2))
+        psum_m = ctx.enter_context(tc.psum_pool(name="psum_m", bufs=2))
+
+        def load(name, rows, cuts):
+            pieces = []
+            for c0, cols, share in cuts:
+                raw = keep.tile([P, 2, cols], F32, name=f"{name}_raw{c0}")
+                nc.sync.dma_start(out=raw[:], in_=rows[:, :, c0 : c0 + cols])
+                pieces.append((raw, c0, cols, share))
+            return pieces
+
+        k_rows = kT.rearrange("(p t) c -> p t c", t=4)
+        x_rows = xq.rearrange("(p t) c -> p t c", t=4)
+        v_rows = vT.rearrange("(p t) c -> p t c", t=2)
+
+        warm = keep.tile([P, 1], F32)
+        nc.gpsimd.memset(warm[:], 0.0)
+        warm_out = keep.tile([P, 1], F32)
+        nc.scalar.activation(out=warm_out[:], in_=warm[:], func=EXP)
+
+        vs_col = keep.tile([P, 16], F32)
+        nc.sync.dma_start(out=vs_col[:], in_=vs[0, :].rearrange("(p c) -> p c", c=16))
+        k_raw = [load("k0", k_rows[:, 0:2, :], FIRST)]
+        offs_t = keep.tile([P, B * LIST], U16)
+        nc.sync.dma_start(offs_t[:], offs)
+        qoffs_t = keep.tile([P, B * LIST], U16)
+        nc.sync.dma_start(qoffs_t[:], qoffs)
+        k_raw.append(load("k1", k_rows[:, 2:4, :], EVEN))
+        x_raw = [load("x0", x_rows[:, 0:2, :], EVEN), load("x1", x_rows[:, 2:4, :], LAST)]
+        v_raw = load("v", v_rows, EVEN)
+
+        ident = keep.tile([P, P], F32)
+        make_identity(nc, ident[:])
+        windows = []
+        for e in range(2):
+            placed = keep.tile([P, T], F32, name=f"placed{e}")
+            nc.gpsimd.memset(placed[:], 0.0)
+            windows.append(placed)
+
+        def pool_tile(name, pieces):
+            pairs = keep.tile([P, T * 2], BF16, name=f"{name}_pairs", align_bytes=64)
+            view = pairs[:].rearrange("p (c t) -> p c t", t=2)
+            for raw, c0, cols, share in pieces:
+                src = raw[:].rearrange("p t c -> p c t")
+                nc.scalar.activation(out=view[:, c0 : c0 + share, :], in_=src[:, 0:share, :], func=COPY)
+                nc.vector.tensor_copy(out=view[:, c0 + share : c0 + cols, :], in_=src[:, share:cols, :])
+            return pairs
+
+        def my_offs(table, b):
+            return table[:, b * LIST : (b + 1) * LIST]
+
+        vs_all = keep.tile([P, T], F32)
+        for g in range(4):
+            bank = psum_m.tile([P, 4, P], F32, name="misc")
+            for c in range(4):
+                nc.tensor.transpose(bank[:, c, :], vs_col[:, 4 * g + c : 4 * g + c + 1].to_broadcast([P, P]), ident[:])
+            nc.vector.tensor_copy(
+                out=vs_all[:].rearrange("p (r c) -> p r c", c=16)[:, :, 4 * g : 4 * g + 4],
+                in_=bank[:].rearrange("p c r -> p r c"),
+            )
+
+        k_got = keep.tile([P, 2 * B * N * 2], BF16, align_bytes=64)
+        for u in range(2):
+            pairs = pool_tile(f"k{u}", k_raw[u])
+            half = k_got[:, u * 2 * B * N : (u + 1) * 2 * B * N]
+            nc.vector.tensor_copy(half.bitcast(U32), pairs[:].bitcast(U32).indirect(offs_t[:]))
+        k_codes, k_scales = [], []
+        k_view = k_got[:].rearrange("p (u b q t e) -> p b q t u e", u=2, b=B, t=4, e=2)
+        for b in range(B):
+            grouped = keep.tile([P, 4 * N], BF16, name=f"k_grouped{b}", align_bytes=64)
+            g_view = grouped[:].rearrange("p (t q u e) -> p q t u e", t=4, u=2, e=2)
+            nc.vector.tensor_copy(out=g_view, in_=k_view[:, b])
+            codes = keep.tile([P, N], U32, name=f"k_codes{b}", align_bytes=64)
+            scales = keep.tile([P, N], U8, name=f"k_scales{b}", align_bytes=64)
+            nc.vector.quantize_mx(out=codes[:].bitcast(FP8X4), scales=scales[:], in_=grouped[:])
+            k_codes.append(codes)
+            k_scales.append(scales)
+
+        vs_turned = []
+        for b in range(B):
+            vs_got = keep.tile([P, N], F32, name=f"vs_got{b}")
+            nc.vector.tensor_copy(vs_got[:], vs_all[:].indirect(my_offs(offs_t, b)))
+            bank = psum_m.tile([P, 4, P], F32, name="misc")
+            for t in range(4):
+                nc.tensor.transpose(bank[:, t, :], vs_got[:, t::4], ident[:])
+            turned = keep.tile([P, 4], F32, name=f"vs_turned{b}")
+            nc.vector.tensor_copy(out=turned[:], in_=bank[:, :, 0])
+            vs_turned.append(turned)
+
+        x_grouped = []
+        for b in range(B):
+            grouped = keep.tile([P, 4 * N], BF16, name=f"x_grouped{b}", align_bytes=64)
+            x_grouped.append(grouped)
+        x_codes, x_scales = [], []
+        for u in range(2):
+            pairs = pool_tile(f"x{u}", x_raw[u])
+            for b in range(B):
+                words = x_grouped[b][:].bitcast(U32)
+                nc.vector.tensor_copy(words[:, u::2], pairs[:].bitcast(U32).indirect(my_offs(qoffs_t, b)))
+                if u == 1:
+                    codes = keep.tile([P, N], U32, name=f"x_codes{b}", align_bytes=64)
+                    scales = keep.tile([P, N], U8, name=f"x_scales{b}", align_bytes=64)
+                    nc.vector.quantize_mx(out=codes[:].bitcast(FP8X4), scales=scales[:], in_=x_grouped[b][:])
+                    x_codes.append(codes)
+                    x_scales.append(scales)
+
+        sums = keep.tile([P, B * 4], F32)
+        w_grouped = []
+        for b in range(B):
+            grouped = keep.tile([P, 4 * N], BF16, name=f"w_grouped{b}", align_bytes=64)
+            w_grouped.append(grouped)
+
+        def scores(b, i):
+            bank = psum_s.tile([P, N], F32, name="score")
+            cols = slice(i * P, (i + 1) * P)
+            nc.tensor.matmul_mx(
+                out=bank[:],
+                lhsT=x_codes[b][:, cols].bitcast(FP8X4),
+                lhsT_scale=x_scales[b][:, cols],
+                rhs=k_codes[b][:].bitcast(FP8X4),
+                rhs_scale=k_scales[b][:],
+                start=True,
+                stop=True,
+            )
+            top = work.tile([P, 1], F32, name="top", bufs=8)
+            nc.vector.tensor_reduce(out=top[:], in_=bank[:], axis=AX, op=MAX, negate=True)
+            p = work.tile([P, N], F32, name="p", bufs=8)
+            j = 4 * b + i
+            nc.scalar.activation(out=p[:], in_=bank[:], func=EXP, bias=top[:], accum_out=sums[:, j : j + 1])
+            return p
+
+        def weights(b, i, p):
+            bank = psum_p.tile([P, 4, P], F32, name="turned_p")
+            for t in range(4):
+                nc.tensor.transpose(bank[:, t, :], p[:, t * P : (t + 1) * P], ident[:])
+            nc.vector.tensor_tensor(
+                w_grouped[b][:, i * N : (i + 1) * N].rearrange("p (q t) -> p q t", t=4),
+                bank[:].rearrange("p t q -> p q t"),
+                vs_turned[b][:].unsqueeze(1).to_broadcast([P, P, 4]),
+                MULT,
+            )
+
+        v_planes = []
+        for j in range(2):
+            plane = keep.tile([P, T], BF16, name=f"v_plane{j}", align_bytes=64)
+            v_planes.append(plane)
+        for raw, c0, cols, share in v_raw:
+            for j in range(2):
+                nc.scalar.activation(out=v_planes[j][:, c0 : c0 + cols], in_=raw[:, j, :], func=COPY)
+        v_codes, v_scales = [], []
+
+        def values(b):
+            got = keep.tile([P, 2 * N], BF16, name=f"v_got{b}", align_bytes=64)
+            for j in range(2):
+                nc.scalar.activation(out=got[:, j::2], in_=v_planes[j][:].indirect(my_offs(offs_t, b)), func=COPY)
+            bank = psum_m.tile([P, 4, P], F32, name="misc")
+            for t in range(4):
+                nc.tensor.transpose(bank[:, t, :], got[:].bitcast(F32)[:, t::4], ident[:])
+            grouped = keep.tile([P, 4 * DV], BF16, name=f"v_grouped{b}", align_bytes=64)
+            nc.scalar.copy(
+                out=grouped[:].rearrange("p (e t) -> p e t", t=4),
+                in_=bank[:].rearrange("p t w -> p (t w)").bitcast(BF16).rearrange("p (t e) -> p e t", t=4),
+            )
+            codes = keep.tile([P, DV], U32, name=f"v_codes{b}", align_bytes=64)
+            scales = keep.tile([P, DV], U8, name=f"v_scales{b}", align_bytes=64)
+            nc.vector.quantize_mx(out=codes[:].bitcast(FP8X4), scales=scales[:], in_=grouped[:])
+            v_codes.append(codes)
+            v_scales.append(scales)
+
+        inverse = keep.tile([P, B * 4], F32)
+        inverse_rows = []
+
+        def invert(b):
+            cols = slice(4 * b, 4 * b + 4)
+            nc.vector.reciprocal(out=inverse[:, cols], in_=sums[:, cols])
+            bank = psum_m.tile([P, 4, P], F32, name="misc")
+            for i in range(4):
+                nc.tensor.transpose(bank[:, i, :], inverse[:, 4 * b + i : 4 * b + i + 1].to_broadcast([P, P]), ident[:])
+            row = keep.tile([P, N], F32, name=f"inverse_row{b}")
+            nc.scalar.copy(out=row[:], in_=bank[:].rearrange("p i q -> p (i q)"))
+            inverse_rows.append(row)
+
+        w_codes, w_scales = [], []
+
+        def quantise_weights(b):
+            codes = keep.tile([P, N], U32, name=f"w_codes{b}", align_bytes=64)
+            scales = keep.tile([P, N], U8, name=f"w_scales{b}", align_bytes=64)
+            nc.vector.quantize_mx(out=codes[:].bitcast(FP8X4), scales=scales[:], in_=w_grouped[b][:])
+            w_codes.append(codes)
+            w_scales.append(scales)
+
+        def outputs(b, e):
+            cols = slice(e * P, (e + 1) * P)
+            bank = psum_m.tile([P, N], F32, name="misc")
+            nc.tensor.matmul_mx(
+                out=bank[:],
+                lhsT=v_codes[b][:, cols].bitcast(FP8X4),
+                lhsT_scale=v_scales[b][:, cols],
+                rhs=w_codes[b][:].bitcast(FP8X4),
+                rhs_scale=w_scales[b][:],
+                start=True,
+                stop=True,
+            )
+            y = work.tile([P, N], F32, name="y", bufs=4)
+            nc.vector.tensor_tensor(y[:], bank[:], inverse_rows[b][:], MULT)
+            nc.vector.tensor_copy(windows[e][:].indirect(my_offs(qoffs_t, b)), y[:])
+            if b == B - 1:
+                nc.sync.dma_start(out=out[e * P : (e + 1) * P, :], in_=windows[e][:])
+
+        turned_p = {}
+        for b in range(B):
+            for i in range(4):
+                turned_p[b, i] = scores(b, i)
+        for b in range(B):
+            for i in range(4):
+                weights(b, i, turned_p[b, i])
+            invert(b)
+            quantise_weights(b)
+            values(b)
+        for b in range(B):
+            for e in range(2):
+                outputs(b, e)

@@ -20,24 +20,26 @@ B, N, T, D, DV = 2, 512, 2048, 512, 256
 FLOPS = 2 * B * N * N * (D + DV)
 LIST = N // 16
 
-EVEN = ((0, 1024, 832), (1024, 1024, 832))
-FIRST = ((0, 512, 352), (512, 512, 416), (1024, 1024, 832))
-LAST = ((0, 1024, 832), (1024, 512, 416), (1536, 256, 160), (1792, 256, 96))
+EVEN = ((0, 1024, 896), (1024, 512, 448), (1536, 512, 384))
+FIRST = ((0, 256, 256), (256, 256, 224), (512, 512, 448), (1024, 512, 448), (1536, 512, 384))
+VALUES = ((0, 512, 512), (512, 512, 512), (1024, 512, 512), (1536, 512, 512))
+LAST = ((0, 512, 448), (512, 512, 448), (1024, 512, 448), (1536, 256, 192), (1792, 256, 96))
+POOL_TILES = ((), ())
 
 
 def tile_attend_cluster_self_kernel(tc, xq, kT, vT, vs, offs, qoffs, out):
     nc = tc.nc
     with ExitStack() as ctx:
         keep = ctx.enter_context(tc.tile_pool(name="keep", bufs=1))
-        work = ctx.enter_context(tc.tile_pool(name="work", bufs=3))
-        psum_s = ctx.enter_context(tc.psum_pool(name="psum_s", bufs=4))
-        psum_p = ctx.enter_context(tc.psum_pool(name="psum_p", bufs=2))
+        work = ctx.enter_context(tc.tile_pool(name="work", bufs=4))
+        psum_s = ctx.enter_context(tc.psum_pool(name="psum_s", bufs=3))
+        psum_p = ctx.enter_context(tc.psum_pool(name="psum_p", bufs=3))
         psum_m = ctx.enter_context(tc.psum_pool(name="psum_m", bufs=2))
 
-        def load(name, rows, cuts):
+        def load(name, rows, cuts, reuse=()):
             pieces = []
             for c0, cols, share in cuts:
-                raw = keep.tile([P, 2, cols], F32, name=f"{name}_raw{c0}")
+                raw = keep.tile([P, 2, cols], F32, name=f"{'k0' if c0 in reuse else name}_raw{c0}")
                 nc.sync.dma_start(out=raw[:], in_=rows[:, :, c0 : c0 + cols])
                 pieces.append((raw, c0, cols, share))
             return pieces
@@ -53,17 +55,18 @@ def tile_attend_cluster_self_kernel(tc, xq, kT, vT, vs, offs, qoffs, out):
 
         vs_col = keep.tile([P, 16], F32)
         nc.sync.dma_start(out=vs_col[:], in_=vs[0, :].rearrange("(p c) -> p c", c=16))
-        k_raw = [load("k0", k_rows[:, 0:2, :], FIRST)]
         offs_t = keep.tile([P, B * LIST], U16)
         nc.sync.dma_start(offs_t[:], offs)
         qoffs_t = keep.tile([P, B * LIST], U16)
         nc.sync.dma_start(qoffs_t[:], qoffs)
-        k_raw.append(load("k1", k_rows[:, 2:4, :], EVEN))
+        k_raw = [load("k0", k_rows[:, 0:2, :], FIRST), load("k1", k_rows[:, 2:4, :], EVEN)]
         x_raw = [load("x0", x_rows[:, 0:2, :], EVEN), load("x1", x_rows[:, 2:4, :], LAST)]
-        v_raw = load("v", v_rows, EVEN)
+        v_raw = load("v", v_rows, VALUES, (512, 1024, 1536))
 
         ident = keep.tile([P, P], F32)
         make_identity(nc, ident[:])
+        ident_bf = keep.tile([P, P], BF16)
+        nc.gpsimd.tensor_copy(out=ident_bf[:], in_=ident[:])
         windows = []
         for e in range(2):
             placed = keep.tile([P, T], F32, name=f"placed{e}")
@@ -76,11 +79,18 @@ def tile_attend_cluster_self_kernel(tc, xq, kT, vT, vs, offs, qoffs, out):
             for raw, c0, cols, share in pieces:
                 src = raw[:].rearrange("p t c -> p c t")
                 nc.scalar.activation(out=view[:, c0 : c0 + share, :], in_=src[:, 0:share, :], func=COPY)
-                nc.vector.tensor_copy(out=view[:, c0 + share : c0 + cols, :], in_=src[:, share:cols, :])
+                if share < cols:
+                    nc.vector.tensor_copy(out=view[:, c0 + share : c0 + cols, :], in_=src[:, share:cols, :])
             return pairs
 
         def my_offs(table, b):
             return table[:, b * LIST : (b + 1) * LIST]
+
+        def quantise(name, grouped, width):
+            codes = keep.tile([P, width], U32, name=f"{name}_codes", align_bytes=64)
+            scales = keep.tile([P, width], U8, name=f"{name}_scales", align_bytes=64)
+            nc.vector.quantize_mx(out=codes[:].bitcast(FP8X4), scales=scales[:], in_=grouped[:])
+            return codes, scales
 
         vs_all = keep.tile([P, T], F32)
         for g in range(4):
@@ -92,27 +102,15 @@ def tile_attend_cluster_self_kernel(tc, xq, kT, vT, vs, offs, qoffs, out):
                 in_=bank[:].rearrange("p c r -> p r c"),
             )
 
-        k_got = keep.tile([P, 2 * B * N * 2], BF16, align_bytes=64)
-        for u in range(2):
-            pairs = pool_tile(f"k{u}", k_raw[u])
-            half = k_got[:, u * 2 * B * N : (u + 1) * 2 * B * N]
-            nc.vector.tensor_copy(half.bitcast(U32), pairs[:].bitcast(U32).indirect(offs_t[:]))
-        k_codes, k_scales = [], []
-        k_view = k_got[:].rearrange("p (u b q t e) -> p b q t u e", u=2, b=B, t=4, e=2)
-        for b in range(B):
-            grouped = keep.tile([P, 4 * N], BF16, name=f"k_grouped{b}", align_bytes=64)
-            g_view = grouped[:].rearrange("p (t q u e) -> p q t u e", t=4, u=2, e=2)
-            nc.vector.tensor_copy(out=g_view, in_=k_view[:, b])
-            codes = keep.tile([P, N], U32, name=f"k_codes{b}", align_bytes=64)
-            scales = keep.tile([P, N], U8, name=f"k_scales{b}", align_bytes=64)
-            nc.vector.quantize_mx(out=codes[:].bitcast(FP8X4), scales=scales[:], in_=grouped[:])
-            k_codes.append(codes)
-            k_scales.append(scales)
-
-        vs_turned = []
+        vs_turned, vs_perm = [], []
         for b in range(B):
             vs_got = keep.tile([P, N], F32, name=f"vs_got{b}")
             nc.vector.tensor_copy(vs_got[:], vs_all[:].indirect(my_offs(offs_t, b)))
+            perm = keep.tile([P, N], F32, name=f"vs_perm{b}")
+            nc.gpsimd.tensor_copy(
+                out=perm[:].rearrange("p (t q) -> p t q", t=4), in_=vs_got[:].rearrange("p (q t) -> p t q", t=4)
+            )
+            vs_perm.append(perm)
             bank = psum_m.tile([P, 4, P], F32, name="misc")
             for t in range(4):
                 nc.tensor.transpose(bank[:, t, :], vs_got[:, t::4], ident[:])
@@ -120,24 +118,33 @@ def tile_attend_cluster_self_kernel(tc, xq, kT, vT, vs, offs, qoffs, out):
             nc.vector.tensor_copy(out=turned[:], in_=bank[:, :, 0])
             vs_turned.append(turned)
 
-        x_grouped = []
+        k_got = keep.tile([P, 2 * B * N * 2], BF16, align_bytes=64)
+        for u in range(2):
+            pairs = pool_tile(f"k{u}", k_raw[u])
+            half = k_got[:, u * 2 * B * N : (u + 1) * 2 * B * N]
+            nc.vector.tensor_copy(half.bitcast(U32), pairs[:].bitcast(U32).indirect(offs_t[:]))
+        k_mx = []
+        k_view = k_got[:].rearrange("p (u b q t e) -> p b q t u e", u=2, b=B, t=4, e=2)
+        for b in range(B):
+            grouped = keep.tile([P, 4 * N], BF16, name=f"k_grouped{b}", align_bytes=64)
+            g_view = grouped[:].rearrange("p (t q u e) -> p q t u e", t=4, u=2, e=2)
+            nc.vector.tensor_copy(out=g_view, in_=k_view[:, b])
+            k_mx.append(quantise(f"k{b}", grouped, N))
+
+        x_grouped, x_mx = [], []
         for b in range(B):
             grouped = keep.tile([P, 4 * N], BF16, name=f"x_grouped{b}", align_bytes=64)
             x_grouped.append(grouped)
-        x_codes, x_scales = [], []
         for u in range(2):
             pairs = pool_tile(f"x{u}", x_raw[u])
             for b in range(B):
                 words = x_grouped[b][:].bitcast(U32)
                 nc.vector.tensor_copy(words[:, u::2], pairs[:].bitcast(U32).indirect(my_offs(qoffs_t, b)))
                 if u == 1:
-                    codes = keep.tile([P, N], U32, name=f"x_codes{b}", align_bytes=64)
-                    scales = keep.tile([P, N], U8, name=f"x_scales{b}", align_bytes=64)
-                    nc.vector.quantize_mx(out=codes[:].bitcast(FP8X4), scales=scales[:], in_=x_grouped[b][:])
-                    x_codes.append(codes)
-                    x_scales.append(scales)
+                    x_mx.append(quantise(f"x{b}", x_grouped[b], N))
 
         sums = keep.tile([P, B * 4], F32)
+        inverse = keep.tile([P, B * 4], F32)
         w_grouped = []
         for b in range(B):
             grouped = keep.tile([P, 4 * N], BF16, name=f"w_grouped{b}", align_bytes=64)
@@ -148,10 +155,10 @@ def tile_attend_cluster_self_kernel(tc, xq, kT, vT, vs, offs, qoffs, out):
             cols = slice(i * P, (i + 1) * P)
             nc.tensor.matmul_mx(
                 out=bank[:],
-                lhsT=x_codes[b][:, cols].bitcast(FP8X4),
-                lhsT_scale=x_scales[b][:, cols],
-                rhs=k_codes[b][:].bitcast(FP8X4),
-                rhs_scale=k_scales[b][:],
+                lhsT=x_mx[b][0][:, cols].bitcast(FP8X4),
+                lhsT_scale=x_mx[b][1][:, cols],
+                rhs=k_mx[b][0][:].bitcast(FP8X4),
+                rhs_scale=k_mx[b][1][:],
                 start=True,
                 stop=True,
             )
@@ -163,29 +170,28 @@ def tile_attend_cluster_self_kernel(tc, xq, kT, vT, vs, offs, qoffs, out):
             return p
 
         def weights(b, i, p):
-            bank = psum_p.tile([P, 4, P], F32, name="turned_p")
-            for t in range(4):
-                nc.tensor.transpose(bank[:, t, :], p[:, t * P : (t + 1) * P], ident[:])
-            nc.vector.tensor_tensor(
-                w_grouped[b][:, i * N : (i + 1) * N].rearrange("p (q t) -> p q t", t=4),
-                bank[:].rearrange("p t q -> p q t"),
-                vs_turned[b][:].unsqueeze(1).to_broadcast([P, P, 4]),
-                MULT,
-            )
-
-        v_planes = []
-        for j in range(2):
-            plane = keep.tile([P, T], BF16, name=f"v_plane{j}", align_bytes=64)
-            v_planes.append(plane)
-        for raw, c0, cols, share in v_raw:
-            for j in range(2):
-                nc.scalar.activation(out=v_planes[j][:, c0 : c0 + cols], in_=raw[:, j, :], func=COPY)
-        v_codes, v_scales = [], []
+            target = w_grouped[b][:, i * N : (i + 1) * N].rearrange("p (q t) -> p q t", t=4)
+            if i in POOL_TILES[b]:
+                w = work.tile([P, N], BF16, name="w")
+                nc.gpsimd.tensor_tensor(w[:], p[:], vs_perm[b][:], MULT)
+                bank = psum_p.tile([P, 4, P], BF16, name="turned_p")
+                for t in range(4):
+                    nc.tensor.transpose(bank[:, t, :], w[:, t * P : (t + 1) * P], ident_bf[:])
+                nc.scalar.copy(out=target, in_=bank[:].rearrange("p t q -> p q t"))
+            else:
+                bank = psum_p.tile([P, 4, P], F32, name="turned_p")
+                for t in range(4):
+                    nc.tensor.transpose(bank[:, t, :], p[:, t * P : (t + 1) * P], ident[:])
+                nc.vector.tensor_tensor(
+                    target,
+                    bank[:].rearrange("p t q -> p q t"),
+                    vs_turned[b][:].unsqueeze(1).to_broadcast([P, P, 4]),
+                    MULT,
+                )
 
         def values(b):
             got = keep.tile([P, 2 * N], BF16, name=f"v_got{b}", align_bytes=64)
-            for j in range(2):
-                nc.scalar.activation(out=got[:, j::2], in_=v_planes[j][:].indirect(my_offs(offs_t, b)), func=COPY)
+            nc.vector.tensor_copy(got[:].bitcast(U32), v_pairs[:].bitcast(U32).indirect(my_offs(offs_t, b)))
             bank = psum_m.tile([P, 4, P], F32, name="misc")
             for t in range(4):
                 nc.tensor.transpose(bank[:, t, :], got[:].bitcast(F32)[:, t::4], ident[:])
@@ -194,14 +200,7 @@ def tile_attend_cluster_self_kernel(tc, xq, kT, vT, vs, offs, qoffs, out):
                 out=grouped[:].rearrange("p (e t) -> p e t", t=4),
                 in_=bank[:].rearrange("p t w -> p (t w)").bitcast(BF16).rearrange("p (t e) -> p e t", t=4),
             )
-            codes = keep.tile([P, DV], U32, name=f"v_codes{b}", align_bytes=64)
-            scales = keep.tile([P, DV], U8, name=f"v_scales{b}", align_bytes=64)
-            nc.vector.quantize_mx(out=codes[:].bitcast(FP8X4), scales=scales[:], in_=grouped[:])
-            v_codes.append(codes)
-            v_scales.append(scales)
-
-        inverse = keep.tile([P, B * 4], F32)
-        inverse_rows = []
+            return quantise(f"v{b}", grouped, DV)
 
         def invert(b):
             cols = slice(4 * b, 4 * b + 4)
@@ -211,45 +210,45 @@ def tile_attend_cluster_self_kernel(tc, xq, kT, vT, vs, offs, qoffs, out):
                 nc.tensor.transpose(bank[:, i, :], inverse[:, 4 * b + i : 4 * b + i + 1].to_broadcast([P, P]), ident[:])
             row = keep.tile([P, N], F32, name=f"inverse_row{b}")
             nc.scalar.copy(out=row[:], in_=bank[:].rearrange("p i q -> p (i q)"))
-            inverse_rows.append(row)
+            return row
 
-        w_codes, w_scales = [], []
+        def products(b, v_mx, w_mx):
+            tiles = []
+            for e in range(2):
+                cols = slice(e * P, (e + 1) * P)
+                bank = psum_m.tile([P, N], F32, name="misc")
+                nc.tensor.matmul_mx(
+                    out=bank[:],
+                    lhsT=v_mx[0][:, cols].bitcast(FP8X4),
+                    lhsT_scale=v_mx[1][:, cols],
+                    rhs=w_mx[0][:].bitcast(FP8X4),
+                    rhs_scale=w_mx[1][:],
+                    start=True,
+                    stop=True,
+                )
+                y = work.tile([P, N], F32, name="y")
+                nc.scalar.copy(out=y[:], in_=bank[:])
+                tiles.append(y)
+            return tiles
 
-        def quantise_weights(b):
-            codes = keep.tile([P, N], U32, name=f"w_codes{b}", align_bytes=64)
-            scales = keep.tile([P, N], U8, name=f"w_scales{b}", align_bytes=64)
-            nc.vector.quantize_mx(out=codes[:].bitcast(FP8X4), scales=scales[:], in_=w_grouped[b][:])
-            w_codes.append(codes)
-            w_scales.append(scales)
-
-        def outputs(b, e):
-            cols = slice(e * P, (e + 1) * P)
-            bank = psum_m.tile([P, N], F32, name="misc")
-            nc.tensor.matmul_mx(
-                out=bank[:],
-                lhsT=v_codes[b][:, cols].bitcast(FP8X4),
-                lhsT_scale=v_scales[b][:, cols],
-                rhs=w_codes[b][:].bitcast(FP8X4),
-                rhs_scale=w_scales[b][:],
-                start=True,
-                stop=True,
-            )
-            y = work.tile([P, N], F32, name="y", bufs=4)
-            nc.vector.tensor_tensor(y[:], bank[:], inverse_rows[b][:], MULT)
-            nc.vector.tensor_copy(windows[e][:].indirect(my_offs(qoffs_t, b)), y[:])
+        def scatter(b, e, y, row):
+            nc.vector.tensor_tensor(windows[e][:].indirect(my_offs(qoffs_t, b)), y[:], row[:], MULT)
             if b == B - 1:
                 nc.sync.dma_start(out=out[e * P : (e + 1) * P, :], in_=windows[e][:])
 
-        turned_p = {}
+        p_of = {}
         for b in range(B):
             for i in range(4):
-                turned_p[b, i] = scores(b, i)
+                p_of[b, i] = scores(b, i)
+        v_pairs = pool_tile("v", v_raw)
+        y_of, rows = [], []
         for b in range(B):
             for i in range(4):
-                weights(b, i, turned_p[b, i])
-            invert(b)
-            quantise_weights(b)
-            values(b)
+                weights(b, i, p_of[b, i])
+            rows.append(invert(b))
+            w_mx = quantise(f"w{b}", w_grouped[b], N)
+            v_mx = values(b)
+            y_of.append(products(b, v_mx, w_mx))
         for b in range(B):
             for e in range(2):
-                outputs(b, e)
+                scatter(b, e, y_of[b][e], rows[b])

@@ -20,11 +20,11 @@ B, N, T, D, DV = 2, 512, 2048, 512, 256
 FLOPS = 2 * B * N * N * (D + DV)
 LIST = N // 16
 
-EVEN = ((0, 1024, 896), (1024, 512, 448), (1536, 512, 384))
-FIRST = ((0, 256, 256), (256, 256, 224), (512, 512, 448), (1024, 512, 448), (1536, 512, 384))
+EVEN = ((0, 512, 512), (512, 512, 512), (1024, 512, 512), (1536, 512, 256))
+FIRST = ((0, 256, 256), (256, 256, 256), (512, 512, 512), (1024, 512, 512), (1536, 512, 192))
 VALUES = ((0, 512, 512), (512, 512, 512), (1024, 512, 512), (1536, 512, 512))
-LAST = ((0, 512, 448), (512, 512, 448), (1024, 512, 448), (1536, 256, 192), (1792, 256, 96))
-POOL_TILES = ((), ())
+LAST = ((0, 512, 512), (512, 512, 512), (1024, 512, 352), (1536, 256, 256), (1792, 256, 64))
+POOL_TILES = ((), (0, 1, 2, 3))
 
 
 def tile_attend_cluster_self_kernel(tc, xq, kT, vT, vs, offs, qoffs, out):
@@ -102,18 +102,13 @@ def tile_attend_cluster_self_kernel(tc, xq, kT, vT, vs, offs, qoffs, out):
                 in_=bank[:].rearrange("p c r -> p r c"),
             )
 
-        vs_turned, vs_perm = [], []
+        vs_got = keep.tile([P, B * N], F32)
+        nc.vector.tensor_copy(vs_got[:], vs_all[:].indirect(offs_t[:]))
+        vs_turned = []
         for b in range(B):
-            vs_got = keep.tile([P, N], F32, name=f"vs_got{b}")
-            nc.vector.tensor_copy(vs_got[:], vs_all[:].indirect(my_offs(offs_t, b)))
-            perm = keep.tile([P, N], F32, name=f"vs_perm{b}")
-            nc.gpsimd.tensor_copy(
-                out=perm[:].rearrange("p (t q) -> p t q", t=4), in_=vs_got[:].rearrange("p (q t) -> p t q", t=4)
-            )
-            vs_perm.append(perm)
             bank = psum_m.tile([P, 4, P], F32, name="misc")
             for t in range(4):
-                nc.tensor.transpose(bank[:, t, :], vs_got[:, t::4], ident[:])
+                nc.tensor.transpose(bank[:, t, :], vs_got[:, b * N + t : (b + 1) * N : 4], ident[:])
             turned = keep.tile([P, 4], F32, name=f"vs_turned{b}")
             nc.vector.tensor_copy(out=turned[:], in_=bank[:, :, 0])
             vs_turned.append(turned)
@@ -123,13 +118,12 @@ def tile_attend_cluster_self_kernel(tc, xq, kT, vT, vs, offs, qoffs, out):
             pairs = pool_tile(f"k{u}", k_raw[u])
             half = k_got[:, u * 2 * B * N : (u + 1) * 2 * B * N]
             nc.vector.tensor_copy(half.bitcast(U32), pairs[:].bitcast(U32).indirect(offs_t[:]))
-        k_mx = []
-        k_view = k_got[:].rearrange("p (u b q t e) -> p b q t u e", u=2, b=B, t=4, e=2)
-        for b in range(B):
-            grouped = keep.tile([P, 4 * N], BF16, name=f"k_grouped{b}", align_bytes=64)
-            g_view = grouped[:].rearrange("p (t q u e) -> p q t u e", t=4, u=2, e=2)
-            nc.vector.tensor_copy(out=g_view, in_=k_view[:, b])
-            k_mx.append(quantise(f"k{b}", grouped, N))
+        k_grouped = keep.tile([P, 4 * B * N], BF16, align_bytes=64)
+        nc.vector.tensor_copy(
+            out=k_grouped[:].rearrange("p (n u e) -> p n u e", u=2, e=2),
+            in_=k_got[:].rearrange("p (u n e) -> p n u e", u=2, e=2),
+        )
+        k_mx = quantise("k", k_grouped, B * N)
 
         x_grouped, x_mx = [], []
         for b in range(B):
@@ -153,12 +147,13 @@ def tile_attend_cluster_self_kernel(tc, xq, kT, vT, vs, offs, qoffs, out):
         def scores(b, i):
             bank = psum_s.tile([P, N], F32, name="score")
             cols = slice(i * P, (i + 1) * P)
+            slots = slice(b * N, (b + 1) * N)
             nc.tensor.matmul_mx(
                 out=bank[:],
                 lhsT=x_mx[b][0][:, cols].bitcast(FP8X4),
                 lhsT_scale=x_mx[b][1][:, cols],
-                rhs=k_mx[b][0][:].bitcast(FP8X4),
-                rhs_scale=k_mx[b][1][:],
+                rhs=k_mx[0][:, slots].bitcast(FP8X4),
+                rhs_scale=k_mx[1][:, slots],
                 start=True,
                 stop=True,
             )
@@ -173,15 +168,15 @@ def tile_attend_cluster_self_kernel(tc, xq, kT, vT, vs, offs, qoffs, out):
             target = w_grouped[b][:, i * N : (i + 1) * N].rearrange("p (q t) -> p q t", t=4)
             if i in POOL_TILES[b]:
                 w = work.tile([P, N], BF16, name="w")
-                nc.gpsimd.tensor_tensor(w[:], p[:], vs_perm[b][:], MULT)
+                nc.gpsimd.tensor_tensor(w[:], p[:], vs_got[:, b * N : (b + 1) * N], MULT)
                 bank = psum_p.tile([P, 4, P], BF16, name="turned_p")
                 for t in range(4):
-                    nc.tensor.transpose(bank[:, t, :], w[:, t * P : (t + 1) * P], ident_bf[:])
+                    nc.tensor.transpose(bank[:, t, :], w[:, t::4], ident_bf[:])
                 nc.scalar.copy(out=target, in_=bank[:].rearrange("p t q -> p q t"))
             else:
                 bank = psum_p.tile([P, 4, P], F32, name="turned_p")
                 for t in range(4):
-                    nc.tensor.transpose(bank[:, t, :], p[:, t * P : (t + 1) * P], ident[:])
+                    nc.tensor.transpose(bank[:, t, :], p[:, t::4], ident[:])
                 nc.vector.tensor_tensor(
                     target,
                     bank[:].rearrange("p t q -> p q t"),

@@ -20,10 +20,10 @@ B, N, T, D, DV = 2, 512, 2048, 512, 256
 FLOPS = 2 * B * N * N * (D + DV)
 LIST = N // 16
 
-EVEN = ((0, 512, 512), (512, 512, 512), (1024, 512, 512), (1536, 512, 256))
-FIRST = ((0, 256, 256), (256, 256, 256), (512, 512, 512), (1024, 512, 512), (1536, 512, 192))
+EVEN = ((0, 512, 512), (512, 512, 512), (1024, 512, 512), (1536, 512, 512))
+FIRST = ((0, 256, 256), (256, 256, 256), (512, 512, 512), (1024, 512, 512), (1536, 512, 512))
 VALUES = ((0, 512, 512), (512, 512, 512), (1024, 512, 512), (1536, 512, 512))
-LAST = ((0, 512, 512), (512, 512, 512), (1024, 512, 352), (1536, 256, 256), (1792, 256, 64))
+LAST = ((0, 512, 512), (512, 512, 512), (1024, 512, 512), (1536, 512, 512))
 POOL_TILES = ((), (0, 1, 2, 3))
 
 
@@ -92,11 +92,13 @@ def tile_attend_cluster_self_kernel(tc, xq, kT, vT, vs, offs, qoffs, out):
             nc.vector.quantize_mx(out=codes[:].bitcast(FP8X4), scales=scales[:], in_=grouped[:])
             return codes, scales
 
-        vs_all = keep.tile([P, T], F32)
+        vs_wide = keep.tile([P, 16, P], F32)
+        nc.vector.tensor_copy(out=vs_wide[:], in_=vs_col[:].unsqueeze(2).to_broadcast([P, 16, P]))
+        vs_all = keep.tile([P, T], F32, name="vs_then_k", align_bytes=64)
         for g in range(4):
             bank = psum_m.tile([P, 4, P], F32, name="misc")
             for c in range(4):
-                nc.tensor.transpose(bank[:, c, :], vs_col[:, 4 * g + c : 4 * g + c + 1].to_broadcast([P, P]), ident[:])
+                nc.tensor.transpose(bank[:, c, :], vs_wide[:, 4 * g + c, :], ident[:])
             nc.vector.tensor_copy(
                 out=vs_all[:].rearrange("p (r c) -> p r c", c=16)[:, :, 4 * g : 4 * g + 4],
                 in_=bank[:].rearrange("p c r -> p r c"),
@@ -113,7 +115,7 @@ def tile_attend_cluster_self_kernel(tc, xq, kT, vT, vs, offs, qoffs, out):
             nc.vector.tensor_copy(out=turned[:], in_=bank[:, :, 0])
             vs_turned.append(turned)
 
-        k_got = keep.tile([P, 2 * B * N * 2], BF16, align_bytes=64)
+        k_got = keep.tile([P, 2 * B * N * 2], BF16, name="vs_then_k", align_bytes=64)
         for u in range(2):
             pairs = pool_tile(f"k{u}", k_raw[u])
             half = k_got[:, u * 2 * B * N : (u + 1) * 2 * B * N]
@@ -157,18 +159,26 @@ def tile_attend_cluster_self_kernel(tc, xq, kT, vT, vs, offs, qoffs, out):
                 start=True,
                 stop=True,
             )
-            top = work.tile([P, 1], F32, name="top", bufs=8)
+            top_name = {(0, 3): "v_got0", (1, 1): "v_got1"}.get((b, i), f"top{b}{i}")
+            top = keep.tile([P, 1], F32, name=top_name, align_bytes=64)
             nc.vector.tensor_reduce(out=top[:], in_=bank[:], axis=AX, op=MAX, negate=True)
-            p = work.tile([P, N], F32, name="p", bufs=8)
+            p = keep.tile([P, 4, P], F32, name="k0_raw1536" if (b, i) == (0, 0) else f"p{b}{i}")
             j = 4 * b + i
-            nc.scalar.activation(out=p[:], in_=bank[:], func=EXP, bias=top[:], accum_out=sums[:, j : j + 1])
+            nc.scalar.activation(
+                out=p[:],
+                in_=bank[:].rearrange("p (t q) -> p t q", t=4) if i in POOL_TILES[b] else bank[:].rearrange("p (q t) -> p t q", t=4),
+                func=EXP,
+                bias=top[:],
+                accum_out=sums[:, j : j + 1],
+            )
             return p
 
         def weights(b, i, p):
             target = w_grouped[b][:, i * N : (i + 1) * N].rearrange("p (q t) -> p q t", t=4)
             if i in POOL_TILES[b]:
                 w = work.tile([P, N], BF16, name="w")
-                nc.gpsimd.tensor_tensor(w[:], p[:], vs_got[:, b * N : (b + 1) * N], MULT)
+                slots = vs_got[:, b * N : (b + 1) * N]
+                nc.gpsimd.tensor_tensor(w[:], p[:].rearrange("p t q -> p (t q)"), slots, MULT)
                 bank = psum_p.tile([P, 4, P], BF16, name="turned_p")
                 for t in range(4):
                     nc.tensor.transpose(bank[:, t, :], w[:, t::4], ident_bf[:])
@@ -176,7 +186,7 @@ def tile_attend_cluster_self_kernel(tc, xq, kT, vT, vs, offs, qoffs, out):
             else:
                 bank = psum_p.tile([P, 4, P], F32, name="turned_p")
                 for t in range(4):
-                    nc.tensor.transpose(bank[:, t, :], p[:, t::4], ident[:])
+                    nc.tensor.transpose(bank[:, t, :], p[:, t, :], ident[:])
                 nc.vector.tensor_tensor(
                     target,
                     bank[:].rearrange("p t q -> p q t"),
@@ -200,9 +210,11 @@ def tile_attend_cluster_self_kernel(tc, xq, kT, vT, vs, offs, qoffs, out):
         def invert(b):
             cols = slice(4 * b, 4 * b + 4)
             nc.vector.reciprocal(out=inverse[:, cols], in_=sums[:, cols])
+            wide = keep.tile([P, 4, P], F32, name="inverse_wide")
+            nc.vector.tensor_copy(out=wide[:], in_=inverse[:, cols].unsqueeze(2).to_broadcast([P, 4, P]))
             bank = psum_m.tile([P, 4, P], F32, name="misc")
             for i in range(4):
-                nc.tensor.transpose(bank[:, i, :], inverse[:, 4 * b + i : 4 * b + i + 1].to_broadcast([P, P]), ident[:])
+                nc.tensor.transpose(bank[:, i, :], wide[:, i, :], ident[:])
             row = keep.tile([P, N], F32, name=f"inverse_row{b}")
             nc.scalar.copy(out=row[:], in_=bank[:].rearrange("p i q -> p (i q)"))
             return row
@@ -231,11 +243,11 @@ def tile_attend_cluster_self_kernel(tc, xq, kT, vT, vs, offs, qoffs, out):
             if b == B - 1:
                 nc.sync.dma_start(out=out[e * P : (e + 1) * P, :], in_=windows[e][:])
 
+        v_pairs = pool_tile("v", v_raw)
         p_of = {}
         for b in range(B):
             for i in range(4):
                 p_of[b, i] = scores(b, i)
-        v_pairs = pool_tile("v", v_raw)
         y_of, rows = [], []
         for b in range(B):
             for i in range(4):

from contextlib import ExitStack

import concourse.mybir as mybir
from concourse.masks import make_identity

F32 = mybir.dt.float32
BF16 = mybir.dt.bfloat16
U32 = mybir.dt.uint32
U16 = mybir.dt.uint16
U8 = mybir.dt.uint8
FP8X4 = mybir.dt.float8_e4m3fn_x4
MULT = mybir.AluOpType.mult
MAX = mybir.AluOpType.max
AX = mybir.AxisListType.X
EXP = mybir.ActivationFunctionType.Exp
COPY = mybir.ActivationFunctionType.Copy

P = 128
B, N, T, D, DV = 2, 512, 2048, 512, 256
FLOPS = 2 * B * N * N * (D + DV)
LIST = N // 16

EVEN = ((0, 512, 512), (512, 512, 512), (1024, 512, 512), (1536, 512, 512))
FIRST = ((0, 256, 256), (256, 256, 256), (512, 512, 512), (1024, 512, 512), (1536, 512, 512))
VALUES = ((0, 512, 512), (512, 512, 512), (1024, 512, 512), (1536, 512, 512))
LAST = ((0, 512, 512), (512, 512, 512), (1024, 512, 512), (1536, 512, 512))
POOL_TILES = ((), (0, 1, 2, 3))


def tile_attend_cluster_self_kernel(tc, xq, kT, vT, vs, offs, qoffs, out):
    nc = tc.nc
    with ExitStack() as ctx:
        keep = ctx.enter_context(tc.tile_pool(name="keep", bufs=1))
        work = ctx.enter_context(tc.tile_pool(name="work", bufs=4))
        psum_s = ctx.enter_context(tc.psum_pool(name="psum_s", bufs=3))
        psum_p = ctx.enter_context(tc.psum_pool(name="psum_p", bufs=3))
        psum_m = ctx.enter_context(tc.psum_pool(name="psum_m", bufs=2))

        def load(name, rows, cuts, reuse=()):
            pieces = []
            for c0, cols, share in cuts:
                raw = keep.tile([P, 2, cols], F32, name=f"{'k0' if c0 in reuse else name}_raw{c0}")
                nc.sync.dma_start(out=raw[:], in_=rows[:, :, c0 : c0 + cols])
                pieces.append((raw, c0, cols, share))
            return pieces

        k_rows = kT.rearrange("(p t) c -> p t c", t=4)
        x_rows = xq.rearrange("(p t) c -> p t c", t=4)
        v_rows = vT.rearrange("(p t) c -> p t c", t=2)

        warm = keep.tile([P, 1], F32)
        nc.gpsimd.memset(warm[:], 0.0)
        warm_out = keep.tile([P, 1], F32)
        nc.scalar.activation(out=warm_out[:], in_=warm[:], func=EXP)

        vs_col = keep.tile([P, 16], F32)
        nc.sync.dma_start(out=vs_col[:], in_=vs[0, :].rearrange("(p c) -> p c", c=16))
        offs_t = keep.tile([P, B * LIST], U16)
        nc.sync.dma_start(offs_t[:], offs)
        qoffs_t = keep.tile([P, B * LIST], U16)
        nc.sync.dma_start(qoffs_t[:], qoffs)
        k_raw = [load("k0", k_rows[:, 0:2, :], FIRST), load("k1", k_rows[:, 2:4, :], EVEN)]
        x_raw = [load("x0", x_rows[:, 0:2, :], EVEN), load("x1", x_rows[:, 2:4, :], LAST)]
        v_raw = load("v", v_rows, VALUES, (512, 1024, 1536))

        ident = keep.tile([P, P], F32)
        make_identity(nc, ident[:])
        ident_bf = keep.tile([P, P], BF16)
        nc.gpsimd.tensor_copy(out=ident_bf[:], in_=ident[:])
        windows = []
        for e in range(2):
            placed = keep.tile([P, T], F32, name=f"placed{e}")
            nc.gpsimd.memset(placed[:], 0.0)
            windows.append(placed)

        def pool_tile(name, pieces):
            pairs = keep.tile([P, T * 2], BF16, name=f"{name}_pairs", align_bytes=64)
            view = pairs[:].rearrange("p (c t) -> p c t", t=2)
            for raw, c0, cols, share in pieces:
                src = raw[:].rearrange("p t c -> p c t")
                nc.scalar.activation(out=view[:, c0 : c0 + share, :], in_=src[:, 0:share, :], func=COPY)
                if share < cols:
                    nc.vector.tensor_copy(out=view[:, c0 + share : c0 + cols, :], in_=src[:, share:cols, :])
            return pairs

        def my_offs(table, b):
            return table[:, b * LIST : (b + 1) * LIST]

        def quantise(name, grouped, width):
            codes = keep.tile([P, width], U32, name=f"{name}_codes", align_bytes=64)
            scales = keep.tile([P, width], U8, name=f"{name}_scales", align_bytes=64)
            nc.vector.quantize_mx(out=codes[:].bitcast(FP8X4), scales=scales[:], in_=grouped[:])
            return codes, scales

        vs_wide = keep.tile([P, 16, P], F32)
        nc.vector.tensor_copy(out=vs_wide[:], in_=vs_col[:].unsqueeze(2).to_broadcast([P, 16, P]))
        vs_all = keep.tile([P, T], F32, name="vs_then_k", align_bytes=64)
        for g in range(4):
            bank = psum_m.tile([P, 4, P], F32, name="misc")
            for c in range(4):
                nc.tensor.transpose(bank[:, c, :], vs_wide[:, 4 * g + c, :], ident[:])
            nc.vector.tensor_copy(
                out=vs_all[:].rearrange("p (r c) -> p r c", c=16)[:, :, 4 * g : 4 * g + 4],
                in_=bank[:].rearrange("p c r -> p r c"),
            )

        vs_got = keep.tile([P, B * N], F32)
        nc.vector.tensor_copy(vs_got[:], vs_all[:].indirect(offs_t[:]))
        vs_turned = []
        for b in range(B):
            bank = psum_m.tile([P, 4, P], F32, name="misc")
            for t in range(4):
                nc.tensor.transpose(bank[:, t, :], vs_got[:, b * N + t : (b + 1) * N : 4], ident[:])
            turned = keep.tile([P, 4], F32, name=f"vs_turned{b}")
            nc.vector.tensor_copy(out=turned[:], in_=bank[:, :, 0])
            vs_turned.append(turned)

        k_got = keep.tile([P, 2 * B * N * 2], BF16, name="vs_then_k", align_bytes=64)
        for u in range(2):
            pairs = pool_tile(f"k{u}", k_raw[u])
            half = k_got[:, u * 2 * B * N : (u + 1) * 2 * B * N]
            nc.vector.tensor_copy(half.bitcast(U32), pairs[:].bitcast(U32).indirect(offs_t[:]))
        k_grouped = keep.tile([P, 4 * B * N], BF16, align_bytes=64)
        nc.vector.tensor_copy(
            out=k_grouped[:].rearrange("p (n u e) -> p n u e", u=2, e=2),
            in_=k_got[:].rearrange("p (u n e) -> p n u e", u=2, e=2),
        )
        k_mx = quantise("k", k_grouped, B * N)

        x_grouped, x_mx = [], []
        for b in range(B):
            grouped = keep.tile([P, 4 * N], BF16, name=f"x_grouped{b}", align_bytes=64)
            x_grouped.append(grouped)
        for u in range(2):
            pairs = pool_tile(f"x{u}", x_raw[u])
            for b in range(B):
                words = x_grouped[b][:].bitcast(U32)
                nc.vector.tensor_copy(words[:, u::2], pairs[:].bitcast(U32).indirect(my_offs(qoffs_t, b)))
                if u == 1:
                    x_mx.append(quantise(f"x{b}", x_grouped[b], N))

        sums = keep.tile([P, B * 4], F32)
        inverse = keep.tile([P, B * 4], F32)
        w_grouped = []
        for b in range(B):
            grouped = keep.tile([P, 4 * N], BF16, name=f"w_grouped{b}", align_bytes=64)
            w_grouped.append(grouped)

        def scores(b, i):
            bank = psum_s.tile([P, N], F32, name="score")
            cols = slice(i * P, (i + 1) * P)
            slots = slice(b * N, (b + 1) * N)
            nc.tensor.matmul_mx(
                out=bank[:],
                lhsT=x_mx[b][0][:, cols].bitcast(FP8X4),
                lhsT_scale=x_mx[b][1][:, cols],
                rhs=k_mx[0][:, slots].bitcast(FP8X4),
                rhs_scale=k_mx[1][:, slots],
                start=True,
                stop=True,
            )
            top_name = {(0, 3): "v_got0", (1, 1): "v_got1"}.get((b, i), f"top{b}{i}")
            top = keep.tile([P, 1], F32, name=top_name, align_bytes=64)
            nc.vector.tensor_reduce(out=top[:], in_=bank[:], axis=AX, op=MAX, negate=True)
            p = keep.tile([P, 4, P], F32, name="k0_raw1536" if (b, i) == (0, 0) else f"p{b}{i}")
            j = 4 * b + i
            nc.scalar.activation(
                out=p[:],
                in_=bank[:].rearrange("p (t q) -> p t q", t=4) if i in POOL_TILES[b] else bank[:].rearrange("p (q t) -> p t q", t=4),
                func=EXP,
                bias=top[:],
                accum_out=sums[:, j : j + 1],
            )
            return p

        def weights(b, i, p):
            target = w_grouped[b][:, i * N : (i + 1) * N].rearrange("p (q t) -> p q t", t=4)
            if i in POOL_TILES[b]:
                w = work.tile([P, N], BF16, name="w")
                slots = vs_got[:, b * N : (b + 1) * N]
                nc.gpsimd.tensor_tensor(w[:], p[:].rearrange("p t q -> p (t q)"), slots, MULT)
                bank = psum_p.tile([P, 4, P], BF16, name="turned_p")
                for t in range(4):
                    nc.tensor.transpose(bank[:, t, :], w[:, t::4], ident_bf[:])
                nc.scalar.copy(out=target, in_=bank[:].rearrange("p t q -> p q t"))
            else:
                bank = psum_p.tile([P, 4, P], F32, name="turned_p")
                for t in range(4):
                    nc.tensor.transpose(bank[:, t, :], p[:, t, :], ident[:])
                nc.vector.tensor_tensor(
                    target,
                    bank[:].rearrange("p t q -> p q t"),
                    vs_turned[b][:].unsqueeze(1).to_broadcast([P, P, 4]),
                    MULT,
                )

        def values(b):
            got = keep.tile([P, 2 * N], BF16, name=f"v_got{b}", align_bytes=64)
            nc.vector.tensor_copy(got[:].bitcast(U32), v_pairs[:].bitcast(U32).indirect(my_offs(offs_t, b)))
            bank = psum_m.tile([P, 4, P], F32, name="misc")
            for t in range(4):
                nc.tensor.transpose(bank[:, t, :], got[:].bitcast(F32)[:, t::4], ident[:])
            grouped = keep.tile([P, 4 * DV], BF16, name=f"v_grouped{b}", align_bytes=64)
            nc.scalar.copy(
                out=grouped[:].rearrange("p (e t) -> p e t", t=4),
                in_=bank[:].rearrange("p t w -> p (t w)").bitcast(BF16).rearrange("p (t e) -> p e t", t=4),
            )
            return quantise(f"v{b}", grouped, DV)

        def invert(b):
            cols = slice(4 * b, 4 * b + 4)
            nc.vector.reciprocal(out=inverse[:, cols], in_=sums[:, cols])
            wide = keep.tile([P, 4, P], F32, name="inverse_wide")
            nc.vector.tensor_copy(out=wide[:], in_=inverse[:, cols].unsqueeze(2).to_broadcast([P, 4, P]))
            bank = psum_m.tile([P, 4, P], F32, name="misc")
            for i in range(4):
                nc.tensor.transpose(bank[:, i, :], wide[:, i, :], ident[:])
            row = keep.tile([P, N], F32, name=f"inverse_row{b}")
            nc.scalar.copy(out=row[:], in_=bank[:].rearrange("p i q -> p (i q)"))
            return row

        def products(b, v_mx, w_mx):
            tiles = []
            for e in range(2):
                cols = slice(e * P, (e + 1) * P)
                bank = psum_m.tile([P, N], F32, name="misc")
                nc.tensor.matmul_mx(
                    out=bank[:],
                    lhsT=v_mx[0][:, cols].bitcast(FP8X4),
                    lhsT_scale=v_mx[1][:, cols],
                    rhs=w_mx[0][:].bitcast(FP8X4),
                    rhs_scale=w_mx[1][:],
                    start=True,
                    stop=True,
                )
                y = work.tile([P, N], F32, name="y")
                nc.scalar.copy(out=y[:], in_=bank[:])
                tiles.append(y)
            return tiles

        def scatter(b, e, y, row):
            nc.vector.tensor_tensor(windows[e][:].indirect(my_offs(qoffs_t, b)), y[:], row[:], MULT)
            if b == B - 1:
                nc.sync.dma_start(out=out[e * P : (e + 1) * P, :], in_=windows[e][:])

        v_pairs = pool_tile("v", v_raw)
        p_of = {}
        for b in range(B):
            for i in range(4):
                p_of[b, i] = scores(b, i)
        y_of, rows = [], []
        for b in range(B):
            for i in range(4):
                weights(b, i, p_of[b, i])
            rows.append(invert(b))
            w_mx = quantise(f"w{b}", w_grouped[b], N)
            v_mx = values(b)
            y_of.append(products(b, v_mx, w_mx))
        for b in range(B):
            for e in range(2):
                scatter(b, e, y_of[b][e], rows[b])
